import numpy as np
import ml_dtypes


def mxq(x, axis, fmt="e4m3"):
    dtype, down = {"e4m3": (ml_dtypes.float8_e4m3fn, 7), "e5m2": (ml_dtypes.float8_e5m2, 14)}[fmt]
    v = np.moveaxis(np.asarray(x, np.float32).astype(ml_dtypes.bfloat16).astype(np.float64), axis, -1)
    blocks = v.reshape(v.shape[:-1] + (-1, 32))
    amax = np.abs(blocks).max(-1, keepdims=True)
    byte = np.maximum(np.where(amax > 0, np.frexp(amax)[1] - 1 + 127, 0) - down, 1)
    scale = np.exp2(byte - 127.0)
    codes = (blocks / scale).astype(np.float32).astype(dtype).astype(np.float64)
    return np.moveaxis((codes * scale).reshape(v.shape), -1, axis)


WIDE = False


def mx_kscale(k):
    if not WIDE:
        return np.ones(k)
    levels = np.array([10, -10, 5, -5, 0])
    if k % 512:
        return np.exp2(np.random.permutation(np.resize(levels, k // 32))).repeat(32)
    a = np.empty((k // 512, 16))
    for p in range(k // 512):
        a[p, :8] = np.random.permutation(np.resize(levels, 8))
        for g in range(8):
            far = levels[np.abs(levels - a[p, g]) >= 10]
            a[p, g + 8] = far[np.random.randint(len(far))]
    return np.exp2(a.ravel()).repeat(32)


BF16 = ml_dtypes.bfloat16


def bf(x):
    return np.asarray(x, np.float32).astype(BF16)


def f64(x):
    return np.asarray(x).astype(np.float64)


E2M1 = np.array([0.0, 0.5, 1.0, 1.5, 2.0, 3.0, 4.0, 6.0, -0.0, -0.5, -1.0, -1.5, -2.0, -3.0, -4.0, -6.0])


def pack_weight(w, fmt):
    k, n = w.shape
    w = f64(bf(w)).reshape(k // 32, 32, n)
    amax = np.abs(w).max(1)
    if fmt == "e4m3":
        byte = np.frexp(amax)[1] - 1 + 127 - 7
    else:
        mant, ex = np.frexp(amax / 6.0)
        byte = np.where(mant > 0.5, ex, ex - 1) + 127
    byte = np.clip(np.where(amax > 0, byte, 1), 1, 254)
    scaled = (w * np.exp2(127.0 - byte)[:, None, :]).reshape(k, n).astype(np.float32)
    by_word = np.ascontiguousarray(scaled.reshape(k // 512, 128, 4, n).transpose(0, 1, 3, 2))
    if fmt == "e4m3":
        words = by_word.astype(ml_dtypes.float8_e4m3fn).view(np.uint8)
    else:
        c = by_word.astype(ml_dtypes.float4_e2m1fn).view(np.uint8) & 0xF
        words = c[..., 0::2] | (c[..., 1::2] << 4)
    return np.ascontiguousarray(words), np.ascontiguousarray(byte.astype(np.uint8).reshape(k // 512, 16, n))


def unpack_weight(words, scales, fmt):
    g, p, n, _ = words.shape
    if fmt == "e4m3":
        vals = np.ascontiguousarray(words).view(ml_dtypes.float8_e4m3fn).astype(np.float64)
    else:
        nib = np.empty((g, p, n, 4), np.uint8)
        nib[..., 0::2] = words & 0xF
        nib[..., 1::2] = words >> 4
        vals = E2M1[nib]
    vals = vals * np.repeat(np.exp2(scales.astype(np.float64) - 127.0), 8, axis=1)[..., None]
    return vals.transpose(0, 1, 3, 2).reshape(g * 512, n)
def pack4(w):
    words, scales = pack_weight(w, "e2m1")
    return words.reshape(words.shape[0], 128, -1), scales


def unpack4(words, scales):
    return unpack_weight(words.reshape(words.shape[0], 128, -1, 2), scales, "e2m1")


M, D, J, H, P = 1024, 1536, 1024, 32, 2048

B = J // H


def setup_inputs():
    s, t = mx_kscale(D), mx_kscale(J)
    queries = np.random.standard_normal((D, M)) * s[:, None]
    books = 0.5 * np.random.standard_normal((D, J)) / np.sqrt(D) / s[:, None] * t
    pick = np.random.randint(0, H, (B, P))
    codes = (np.arange(H)[None, :, None] == pick[:, None, :]).reshape(J, P) / t[:, None]
    query_words, query_scales = pack4(queries)
    book_words, book_scales = pack4(books)
    code_words, code_scales = pack_weight(codes, "e4m3")
    return {"query_words": query_words, "query_scales": query_scales,
            "book_words": book_words, "book_scales": book_scales,
            "norms": bf(0.2 * np.random.standard_normal(J) * t),
            "caps": bf(0.5 * (1 + 0.1 * np.random.standard_normal(J)) * t),
            "code_words": code_words, "code_scales": code_scales,
            "cross": bf(0.5 * np.random.standard_normal(P))}


def reference(query_words, query_scales, book_words, book_scales, norms, caps, code_words, code_scales, cross):
    queries = unpack4(query_words, query_scales)
    books = unpack4(book_words, book_scales)
    codes = unpack_weight(code_words, code_scales, "e4m3")
    dots = queries.T @ books
    table = np.minimum(dots + f64(norms), f64(caps))
    scan = mxq(table, 1, "e4m3") @ codes
    return scan + f64(cross)

@@ -1,0 +1,209 @@
+from contextlib import ExitStack
+
+import concourse.mybir as mybir
+
+M, D, J, DOCS = 1024, 1536, 1024, 2048
+FLOPS = 2 * M * D * J + 2 * M * J * DOCS
+
+F32 = mybir.dt.float32
+BF16 = mybir.dt.bfloat16
+I32 = mybir.dt.int32
+U32 = mybir.dt.uint32
+U8 = mybir.dt.uint8
+FP8X4 = mybir.dt.float8_e4m3fn_x4
+FP4X4 = mybir.dt.float4_e2m1fn_x4
+ALU = mybir.AluOpType
+
+P = 128
+PACK = 4
+K_PASS = P * PACK
+D_PASSES = D // K_PASS
+J_PASSES = J // K_PASS
+BANK = 512
+BANKS = 8
+CHUNKS = M // BANK
+UNITS = J_PASSES * PACK
+M_TILES = M // P
+TILES_PER_CHUNK = BANK // P
+DOC_BLOCKS = DOCS // BANK
+DOC_HALF = DOCS // 2
+RUN = 4
+PERMUTE_LEAD = 5
+INTERLEAVE_LEAD = 6
+QUANTIZE_LEAD = 3
+
+
+def tensor_steps():
+    steps = [("table", 0, u) for u in range(UNITS)]
+    steps.extend(("table", 1, u) for u in range(PACK))
+    for block in range(M_TILES * DOC_BLOCKS):
+        steps.append(("scan", block // DOC_BLOCKS, block % DOC_BLOCKS))
+        if block % 2 == 1 and PACK + block // 2 < UNITS:
+            steps.append(("table", 1, PACK + block // 2))
+    return steps
+
+
+def tile_additive_quantisation_scan_s4_kernel(
+    tc, query_words, query_scales, book_words, book_scales, norms, caps, code_words, code_scales, cross, out
+):
+    nc = tc.nc
+    with ExitStack() as ctx:
+        keep = ctx.enter_context(tc.tile_pool(name="keep", bufs=1))
+        stage = ctx.enter_context(tc.tile_pool(name="stage", bufs=4))
+        psum = ctx.enter_context(tc.psum_pool(name="psum", bufs=1))
+        ctx.enter_context(tc.manual_schedule())
+
+        def kept(name, shape, dtype):
+            return keep.tile(shape, dtype, name=name, align_bytes=64)
+
+        book_raw = [kept("book_raw%d" % g, [P, D_PASSES, 2 * K_PASS], U8) for g in range(J_PASSES)]
+        book_scale_raw = [kept("book_scale_raw%d" % g, [P, D_PASSES, K_PASS], U8) for g in range(J_PASSES)]
+        book = [kept("book%d" % u, [P, D_PASSES, 2 * P], U8) for u in range(UNITS)]
+        book_scale = [kept("book_scale%d" % u, [P, D_PASSES, P], U8) for u in range(UNITS)]
+        query = [kept("query%d" % c, [P, D_PASSES, 2 * BANK], U8) for c in range(CHUNKS)]
+        query_scale = [kept("query_scale%d" % c, [P, D_PASSES, BANK], U8) for c in range(CHUNKS)]
+        code = [kept("code%d" % h, [P, J_PASSES, DOC_HALF], U32) for h in range(2)]
+        code_scale = kept("code_scale", [P, J_PASSES, DOCS], U8)
+        norm_cols = kept("norm_cols", [P, J_PASSES, PACK], BF16)
+        cap_cols = kept("cap_cols", [P, J_PASSES, PACK], BF16)
+        cross_rows = kept("cross_rows", [P, DOCS], BF16)
+        table_rows = [kept("table_rows%d" % c, [P, UNITS, BANK], BF16) for c in range(CHUNKS)]
+        table_words = [kept("table_words%d" % i, [P, J_PASSES, P, PACK], BF16) for i in range(M_TILES)]
+        table_code = [kept("table_code%d" % i, [P, J_PASSES, P], U32) for i in range(M_TILES)]
+        table_scale = [kept("table_scale%d" % i, [P, J_PASSES, P], U8) for i in range(M_TILES)]
+        result = [kept("result%d" % i, [P, DOCS], F32) for i in range(M_TILES)]
+
+        def load_words(queue, tile, words, part):
+            width = tile.shape[2] // 4
+            src = words.bitcast(I32).rearrange("g p w -> p g w")
+            queue.dma_start(out=tile[:].bitcast(I32), in_=src[:, :, part * width : (part + 1) * width])
+
+        def load_scale_rows(queues, tile, scales, part):
+            width = tile.shape[2] // 4
+            src = scales.bitcast(I32).rearrange("g q w -> q g w")
+            for quadrant in range(4):
+                queues[quadrant % len(queues)].dma_start(
+                    out=tile[:].bitcast(I32)[32 * quadrant : 32 * quadrant + 4],
+                    in_=src[4 * quadrant : 4 * quadrant + 4, :, part * width : (part + 1) * width],
+                )
+
+        for plane in (book_scale_raw[0], query_scale[0], book_scale_raw[1], query_scale[1], code_scale):
+            nc.vector.memset(plane[:].bitcast(I32), 0)
+
+        nc.gpsimd.dma_start(out=norm_cols[:], in_=norms.rearrange("(g p t) -> p g t", p=P, t=PACK))
+        nc.gpsimd.dma_start(out=cap_cols[:], in_=caps.rearrange("(g p t) -> p g t", p=P, t=PACK))
+
+        both = (nc.sync, nc.scalar)
+        load_words(nc.sync, book_raw[0], book_words, 0)
+        load_words(nc.scalar, query[0], query_words, 0)
+        load_scale_rows(both, book_scale_raw[0], book_scales, 0)
+        load_scale_rows(both, query_scale[0], query_scales, 0)
+        load_words(nc.sync, book_raw[1], book_words, 1)
+        load_scale_rows((nc.sync,), book_scale_raw[1], book_scales, 1)
+        load_words(nc.sync, query[1], query_words, 1)
+        load_scale_rows((nc.sync,), query_scale[1], query_scales, 1)
+        load_scale_rows((nc.sync,), code_scale, code_scales, 0)
+        code_src = code_words.rearrange("g p n t -> p g (n t)").bitcast(I32)
+        for h in range(2):
+            nc.sync.dma_start(out=code[h][:].bitcast(I32), in_=code_src[:, :, h * DOC_HALF : (h + 1) * DOC_HALF])
+        nc.sync.dma_start(out=cross_rows[:], in_=cross.partition_broadcast(P))
+
+        def permute_books(u):
+            g, t = divmod(u, PACK)
+            nc.vector.tensor_copy(
+                out=book[u][:].rearrange("p d (c b) -> p d c b", b=2),
+                in_=book_raw[g][:].rearrange("p d (c t b) -> p d c t b", t=PACK, b=2)[:, :, :, t, :],
+            )
+            nc.vector.tensor_copy(
+                out=book_scale[u][:],
+                in_=book_scale_raw[g][:].rearrange("p d (c t) -> p d c t", t=PACK)[:, :, :, t],
+            )
+
+        def table_matmul(acc, c, u):
+            for d in range(D_PASSES):
+                nc.tensor.matmul_mx(
+                    out=acc[:],
+                    lhsT=book[u][:, d, :].bitcast(FP4X4),
+                    lhsT_scale=book_scale[u][:, d, :],
+                    rhs=query[c][:, d, :].bitcast(FP4X4),
+                    rhs_scale=query_scale[c][:, d, :],
+                    start=(d == 0),
+                    stop=(d == D_PASSES - 1),
+                )
+
+        def truncate(dots, c, u):
+            g, t = divmod(u, PACK)
+            nc.vector.tensor_scalar(
+                out=table_rows[c][:, u, :],
+                in0=dots[:],
+                scalar1=norm_cols[:, g, t : t + 1],
+                scalar2=cap_cols[:, g, t : t + 1],
+                op0=ALU.add,
+                op1=ALU.min,
+            )
+
+        def interleave(i):
+            c, k = divmod(i, TILES_PER_CHUNK)
+            src = table_rows[c][:].rearrange("p (g t) m -> p g t m", t=PACK)[:, :, :, k * P : (k + 1) * P]
+            nc.scalar.copy(
+                out=table_words[i][:].rearrange("p g (a r) t -> p g a t r", r=RUN),
+                in_=src.rearrange("p g t (a r) -> p g a t r", r=RUN),
+            )
+
+        def quantize(i):
+            nc.vector.quantize_mx(
+                out=table_code[i][:].rearrange("p g m -> p (g m)").bitcast(FP8X4),
+                scales=table_scale[i][:].rearrange("p g m -> p (g m)"),
+                in_=table_words[i][:].rearrange("p g m t -> p (g m t)"),
+            )
+
+        def scan_matmul(acc, i, n):
+            h, k = divmod(n, DOC_HALF // BANK)
+            for g in range(J_PASSES):
+                nc.tensor.matmul_mx(
+                    out=acc[:],
+                    lhsT=table_code[i][:, g, :].bitcast(FP8X4),
+                    lhsT_scale=table_scale[i][:, g, :],
+                    rhs=code[h][:, g, k * BANK : (k + 1) * BANK].bitcast(FP8X4),
+                    rhs_scale=code_scale[:, g, n * BANK : (n + 1) * BANK],
+                    start=(g == 0),
+                    stop=(g == J_PASSES - 1),
+                )
+
+        def add_cross_and_store(acc, i, n):
+            cols = slice(n * BANK, (n + 1) * BANK)
+            nc.vector.tensor_tensor(out=result[i][:, cols], in0=acc[:], in1=cross_rows[:, cols], op=ALU.add)
+            blocks = 1 if i == M_TILES - 1 else 2
+            if (n + 1) % blocks == 0:
+                done = slice((n + 1 - blocks) * BANK, (n + 1) * BANK)
+                nc.sync.dma_start(out=out[i * P : (i + 1) * P, done], in_=result[i][:, done])
+
+        steps = tensor_steps()
+        first_use = [steps.index(("scan", i, 0)) for i in range(M_TILES)]
+        complete = [steps.index(("table", i // TILES_PER_CHUNK, UNITS - 1)) + 1 for i in range(M_TILES)]
+        interleave_at = {max(complete[i], first_use[i] - INTERLEAVE_LEAD): i for i in range(M_TILES)}
+        quantize_at = {first_use[i] - QUANTIZE_LEAD: i for i in range(M_TILES)}
+
+        for u in range(PERMUTE_LEAD):
+            permute_books(u)
+        pending = None
+        for s, (kind, a, b) in enumerate(steps):
+            if s in quantize_at:
+                quantize(quantize_at[s])
+            acc = psum.tile([P, BANK], F32, name="acc%d" % (s % BANKS), tag="acc%d" % (s % BANKS))
+            if kind == "table":
+                table_matmul(acc, a, b)
+            else:
+                scan_matmul(acc, a, b)
+                add_cross_and_store(acc, a, b)
+            if pending is not None:
+                truncate(*pending)
+                pending = None
+            if s + PERMUTE_LEAD - 1 < UNITS and s >= 1:
+                permute_books(s + PERMUTE_LEAD - 1)
+            if s in interleave_at:
+                interleave(interleave_at[s])
+            if kind == "table":
+                dots = stage.tile([P, BANK], F32, name="dots")
+                nc.scalar.copy(out=dots[:], in_=acc[:])
+                pending = (dots, a, b)

@@ -21,26 +21,33 @@ D_PASSES = D // K_PASS
 J_PASSES = J // K_PASS
 BANK = 512
 BANKS = 8
-CHUNKS = M // BANK
+HALVES = M // BANK
+CHUNK_START = (0, 512, 768)
+CHUNK_WIDTH = (512, 256, 256)
 UNITS = J_PASSES * PACK
 M_TILES = M // P
-TILES_PER_CHUNK = BANK // P
 DOC_BLOCKS = DOCS // BANK
 DOC_HALF = DOCS // 2
 RUN = 4
 PERMUTE_LEAD = 5
-INTERLEAVE_LEAD = 6
-QUANTIZE_LEAD = 3
+
+
+def table_steps(c):
+    per_bank = BANK // CHUNK_WIDTH[c]
+    return [("table", c, u) for u in range(0, UNITS, per_bank)]
 
 
 def tensor_steps():
-    steps = [("table", 0, u) for u in range(UNITS)]
-    steps.extend(("table", 1, u) for u in range(PACK))
-    for block in range(M_TILES * DOC_BLOCKS):
-        steps.append(("scan", block // DOC_BLOCKS, block % DOC_BLOCKS))
-        if block % 2 == 1 and PACK + block // 2 < UNITS:
-            steps.append(("table", 1, PACK + block // 2))
+    steps = table_steps(0) + table_steps(1)
+    late = table_steps(2)
+    for i in range(M_TILES):
+        steps.extend(("scan", i, n) for n in range(DOC_BLOCKS))
+        steps.extend(late[i : i + 1])
     return steps
+
+
+def chunk_of(i):
+    return max(c for c in range(len(CHUNK_START)) if CHUNK_START[c] <= i * P)
 
 
 def tile_additive_quantisation_scan_s4_kernel(
@@ -57,17 +64,17 @@ def tile_additive_quantisation_scan_s4_kernel(
             return keep.tile(shape, dtype, name=name, align_bytes=64)
 
         book_raw = [kept("book_raw%d" % g, [P, D_PASSES, 2 * K_PASS], U8) for g in range(J_PASSES)]
-        book_scale_raw = [kept("book_scale_raw%d" % g, [P, D_PASSES, K_PASS], U8) for g in range(J_PASSES)]
+        book_scale_raw = kept("book_scale_raw", [P, D_PASSES, J], U8)
         book = [kept("book%d" % u, [P, D_PASSES, 2 * P], U8) for u in range(UNITS)]
         book_scale = [kept("book_scale%d" % u, [P, D_PASSES, P], U8) for u in range(UNITS)]
-        query = [kept("query%d" % c, [P, D_PASSES, 2 * BANK], U8) for c in range(CHUNKS)]
-        query_scale = [kept("query_scale%d" % c, [P, D_PASSES, BANK], U8) for c in range(CHUNKS)]
+        query = [kept("query%d" % c, [P, D_PASSES, 2 * BANK], U8) for c in range(HALVES)]
+        query_scale = [kept("query_scale%d" % c, [P, D_PASSES, BANK], U8) for c in range(HALVES)]
         code = [kept("code%d" % h, [P, J_PASSES, DOC_HALF], U32) for h in range(2)]
         code_scale = kept("code_scale", [P, J_PASSES, DOCS], U8)
         norm_cols = kept("norm_cols", [P, J_PASSES, PACK], BF16)
         cap_cols = kept("cap_cols", [P, J_PASSES, PACK], BF16)
         cross_rows = kept("cross_rows", [P, DOCS], BF16)
-        table_rows = [kept("table_rows%d" % c, [P, UNITS, BANK], BF16) for c in range(CHUNKS)]
+        table_rows = [kept("table_rows%d" % c, [P, UNITS, w], BF16) for c, w in enumerate(CHUNK_WIDTH)]
         table_words = [kept("table_words%d" % i, [P, J_PASSES, P, PACK], BF16) for i in range(M_TILES)]
         table_code = [kept("table_code%d" % i, [P, J_PASSES, P], U32) for i in range(M_TILES)]
         table_scale = [kept("table_scale%d" % i, [P, J_PASSES, P], U8) for i in range(M_TILES)]
@@ -87,19 +94,17 @@ def tile_additive_quantisation_scan_s4_kernel(
                     in_=src[4 * quadrant : 4 * quadrant + 4, :, part * width : (part + 1) * width],
                 )
 
-        for plane in (book_scale_raw[0], query_scale[0], book_scale_raw[1], query_scale[1], code_scale):
+        for plane in (book_scale_raw, query_scale[0], query_scale[1], code_scale):
             nc.vector.memset(plane[:].bitcast(I32), 0)
-
-        nc.gpsimd.dma_start(out=norm_cols[:], in_=norms.rearrange("(g p t) -> p g t", p=P, t=PACK))
-        nc.gpsimd.dma_start(out=cap_cols[:], in_=caps.rearrange("(g p t) -> p g t", p=P, t=PACK))
 
         both = (nc.sync, nc.scalar)
         load_words(nc.sync, book_raw[0], book_words, 0)
         load_words(nc.scalar, query[0], query_words, 0)
-        load_scale_rows(both, book_scale_raw[0], book_scales, 0)
+        load_scale_rows(both, book_scale_raw, book_scales, 0)
         load_scale_rows(both, query_scale[0], query_scales, 0)
         load_words(nc.sync, book_raw[1], book_words, 1)
-        load_scale_rows((nc.sync,), book_scale_raw[1], book_scales, 1)
+        nc.sync.dma_start(out=norm_cols[:], in_=norms.rearrange("(g p t) -> p g t", p=P, t=PACK))
+        nc.sync.dma_start(out=cap_cols[:], in_=caps.rearrange("(g p t) -> p g t", p=P, t=PACK))
         load_words(nc.sync, query[1], query_words, 1)
         load_scale_rows((nc.sync,), query_scale[1], query_scales, 1)
         load_scale_rows((nc.sync,), code_scale, code_scales, 0)
@@ -116,17 +121,19 @@ def tile_additive_quantisation_scan_s4_kernel(
             )
             nc.vector.tensor_copy(
                 out=book_scale[u][:],
-                in_=book_scale_raw[g][:].rearrange("p d (c t) -> p d c t", t=PACK)[:, :, :, t],
+                in_=book_scale_raw[:].rearrange("p d (g c t) -> p d g c t", g=J_PASSES, t=PACK)[:, :, g, :, t],
             )
 
         def table_matmul(acc, c, u):
+            half, first = divmod(CHUNK_START[c], BANK)
+            last = first + CHUNK_WIDTH[c]
             for d in range(D_PASSES):
                 nc.tensor.matmul_mx(
-                    out=acc[:],
+                    out=acc,
                     lhsT=book[u][:, d, :].bitcast(FP4X4),
                     lhsT_scale=book_scale[u][:, d, :],
-                    rhs=query[c][:, d, :].bitcast(FP4X4),
-                    rhs_scale=query_scale[c][:, d, :],
+                    rhs=query[half][:, d, 2 * first : 2 * last].bitcast(FP4X4),
+                    rhs_scale=query_scale[half][:, d, first:last],
                     start=(d == 0),
                     stop=(d == D_PASSES - 1),
                 )
@@ -135,7 +142,7 @@ def tile_additive_quantisation_scan_s4_kernel(
             g, t = divmod(u, PACK)
             nc.vector.tensor_scalar(
                 out=table_rows[c][:, u, :],
-                in0=dots[:],
+                in0=dots,
                 scalar1=norm_cols[:, g, t : t + 1],
                 scalar2=cap_cols[:, g, t : t + 1],
                 op0=ALU.add,
@@ -143,8 +150,9 @@ def tile_additive_quantisation_scan_s4_kernel(
             )
 
         def interleave(i):
-            c, k = divmod(i, TILES_PER_CHUNK)
-            src = table_rows[c][:].rearrange("p (g t) m -> p g t m", t=PACK)[:, :, :, k * P : (k + 1) * P]
+            c = chunk_of(i)
+            first = i * P - CHUNK_START[c]
+            src = table_rows[c][:].rearrange("p (g t) m -> p g t m", t=PACK)[:, :, :, first : first + P]
             nc.scalar.copy(
                 out=table_words[i][:].rearrange("p g (a r) t -> p g a t r", r=RUN),
                 in_=src.rearrange("p g t (a r) -> p g a t r", r=RUN),
@@ -172,27 +180,36 @@ def tile_additive_quantisation_scan_s4_kernel(
 
         def add_cross_and_store(acc, i, n):
             cols = slice(n * BANK, (n + 1) * BANK)
-            nc.vector.tensor_tensor(out=result[i][:, cols], in0=acc[:], in1=cross_rows[:, cols], op=ALU.add)
+            if n == 0 and i < M_TILES - 2:
+                nc.scalar.copy(out=result[i][:, cols], in_=acc[:])
+                nc.gpsimd.tensor_tensor(
+                    out=result[i][:, cols], in0=result[i][:, cols], in1=cross_rows[:, cols], op=ALU.add
+                )
+            else:
+                nc.vector.tensor_tensor(out=result[i][:, cols], in0=acc[:], in1=cross_rows[:, cols], op=ALU.add)
             blocks = 1 if i == M_TILES - 1 else 2
             if (n + 1) % blocks == 0:
                 done = slice((n + 1 - blocks) * BANK, (n + 1) * BANK)
                 nc.sync.dma_start(out=out[i * P : (i + 1) * P, done], in_=result[i][:, done])
 
         steps = tensor_steps()
-        first_use = [steps.index(("scan", i, 0)) for i in range(M_TILES)]
-        complete = [steps.index(("table", i // TILES_PER_CHUNK, UNITS - 1)) + 1 for i in range(M_TILES)]
-        interleave_at = {max(complete[i], first_use[i] - INTERLEAVE_LEAD): i for i in range(M_TILES)}
-        quantize_at = {first_use[i] - QUANTIZE_LEAD: i for i in range(M_TILES)}
+        interleave_at = {steps.index(("scan", i - 2, 0)): (i,) for i in range(2, M_TILES)}
+        interleave_at[UNITS] = (0, 1)
+        quantize_at = {steps.index(("scan", i - 1, 1)): (i,) for i in range(1, M_TILES)}
+        quantize_at[UNITS + 1] = (0,)
 
         for u in range(PERMUTE_LEAD):
             permute_books(u)
         pending = None
         for s, (kind, a, b) in enumerate(steps):
-            if s in quantize_at:
-                quantize(quantize_at[s])
+            for i in quantize_at.get(s, ()):
+                quantize(i)
             acc = psum.tile([P, BANK], F32, name="acc%d" % (s % BANKS), tag="acc%d" % (s % BANKS))
             if kind == "table":
-                table_matmul(acc, a, b)
+                width = CHUNK_WIDTH[a]
+                parts = [acc[:, k * width : (k + 1) * width] for k in range(BANK // width)]
+                for k, part in enumerate(parts):
+                    table_matmul(part, a, b + k)
             else:
                 scan_matmul(acc, a, b)
                 add_cross_and_store(acc, a, b)
@@ -201,9 +218,12 @@ def tile_additive_quantisation_scan_s4_kernel(
                 pending = None
             if s + PERMUTE_LEAD - 1 < UNITS and s >= 1:
                 permute_books(s + PERMUTE_LEAD - 1)
-            if s in interleave_at:
-                interleave(interleave_at[s])
-            if kind == "table":
+            for i in interleave_at.get(s, ()):
+                interleave(i)
+            if kind == "table" and a == 0:
                 dots = stage.tile([P, BANK], F32, name="dots")
                 nc.scalar.copy(out=dots[:], in_=acc[:])
-                pending = (dots, a, b)
+                pending = (dots[:], a, b)
+            elif kind == "table":
+                for k, part in enumerate(parts):
+                    truncate(part, a, b + k)

@@ -1,6 +1,7 @@
 from contextlib import ExitStack
 
 import concourse.mybir as mybir
+from concourse.masks import make_identity
 
 M, D, J, DOCS = 1024, 1536, 1024, 2048
 FLOPS = 2 * M * D * J + 2 * M * J * DOCS
@@ -28,8 +29,7 @@ UNITS = J_PASSES * PACK
 M_TILES = M // P
 DOC_BLOCKS = DOCS // BANK
 DOC_HALF = DOCS // 2
-RUN = 4
-PERMUTE_LEAD = 5
+WARM_PASSES = 14
 
 
 def table_steps(c):
@@ -56,7 +56,7 @@ def tile_additive_quantisation_scan_s4_kernel(
     nc = tc.nc
     with ExitStack() as ctx:
         keep = ctx.enter_context(tc.tile_pool(name="keep", bufs=1))
-        stage = ctx.enter_context(tc.tile_pool(name="stage", bufs=4))
+        stage = ctx.enter_context(tc.tile_pool(name="stage", bufs=UNITS))
         psum = ctx.enter_context(tc.psum_pool(name="psum", bufs=1))
         ctx.enter_context(tc.manual_schedule())
 
@@ -64,7 +64,7 @@ def tile_additive_quantisation_scan_s4_kernel(
             return keep.tile(shape, dtype, name=name, align_bytes=64)
 
         book_raw = [kept("book_raw%d" % g, [P, D_PASSES, 2 * K_PASS], U8) for g in range(J_PASSES)]
-        book_scale_raw = kept("book_scale_raw", [P, D_PASSES, J], U8)
+        book_scale_raw = [kept("book_scale_raw%d" % g, [P, D_PASSES, K_PASS], U8) for g in range(J_PASSES)]
         book = [kept("book%d" % u, [P, D_PASSES, 2 * P], U8) for u in range(UNITS)]
         book_scale = [kept("book_scale%d" % u, [P, D_PASSES, P], U8) for u in range(UNITS)]
         query = [kept("query%d" % c, [P, D_PASSES, 2 * BANK], U8) for c in range(HALVES)]
@@ -85,33 +85,71 @@ def tile_additive_quantisation_scan_s4_kernel(
             src = words.bitcast(I32).rearrange("g p w -> p g w")
             queue.dma_start(out=tile[:].bitcast(I32), in_=src[:, :, part * width : (part + 1) * width])
 
-        def load_scale_rows(queues, tile, scales, part):
+        def load_scale_rows(tile, scales, part):
             width = tile.shape[2] // 4
             src = scales.bitcast(I32).rearrange("g q w -> q g w")
             for quadrant in range(4):
-                queues[quadrant % len(queues)].dma_start(
+                nc.sync.dma_start(
                     out=tile[:].bitcast(I32)[32 * quadrant : 32 * quadrant + 4],
                     in_=src[4 * quadrant : 4 * quadrant + 4, :, part * width : (part + 1) * width],
                 )
 
-        for plane in (book_scale_raw, query_scale[0], query_scale[1], code_scale):
-            nc.vector.memset(plane[:].bitcast(I32), 0)
+        def clear(engine, plane):
+            engine.memset(plane[:].bitcast(I32), 0)
 
-        both = (nc.sync, nc.scalar)
-        load_words(nc.sync, book_raw[0], book_words, 0)
-        load_words(nc.scalar, query[0], query_words, 0)
-        load_scale_rows(both, book_scale_raw, book_scales, 0)
-        load_scale_rows(both, query_scale[0], query_scales, 0)
-        load_words(nc.sync, book_raw[1], book_words, 1)
-        nc.sync.dma_start(out=norm_cols[:], in_=norms.rearrange("(g p t) -> p g t", p=P, t=PACK))
-        nc.sync.dma_start(out=cap_cols[:], in_=caps.rearrange("(g p t) -> p g t", p=P, t=PACK))
-        load_words(nc.sync, query[1], query_words, 1)
-        load_scale_rows((nc.sync,), query_scale[1], query_scales, 1)
-        load_scale_rows((nc.sync,), code_scale, code_scales, 0)
-        code_src = code_words.rearrange("g p n t -> p g (n t)").bitcast(I32)
-        for h in range(2):
-            nc.sync.dma_start(out=code[h][:].bitcast(I32), in_=code_src[:, :, h * DOC_HALF : (h + 1) * DOC_HALF])
-        nc.sync.dma_start(out=cross_rows[:], in_=cross.partition_broadcast(P))
+        clear(nc.vector, book_scale_raw[0])
+        clear(nc.vector, query_scale[0])
+        warm_in = kept("warm_in", [P, PACK * P], BF16)
+        warm_code = kept("warm_code", [P, P], U32)
+        warm_scale = kept("warm_scale", [P, P], U8)
+        nc.vector.memset(warm_in[:], 0.0)
+        nc.vector.quantize_mx(out=warm_code[:].bitcast(FP8X4), scales=warm_scale[:], in_=warm_in[:])
+        warm_acc = psum.tile([P, BANK], F32, name="warm_acc", tag="acc%d" % (BANKS - 1))
+        for k in range(WARM_PASSES):
+            nc.tensor.matmul_mx(
+                out=warm_acc[:, :P],
+                lhsT=warm_code[:].bitcast(FP8X4),
+                lhsT_scale=warm_scale[:],
+                rhs=warm_code[:].bitcast(FP8X4),
+                rhs_scale=warm_scale[:],
+                start=(k == 0),
+                stop=(k == WARM_PASSES - 1),
+            )
+        clear(nc.vector, book_scale_raw[1])
+        clear(nc.vector, query_scale[1])
+        clear(nc.vector, code_scale)
+
+        def load_code_words(h):
+            src = code_words.rearrange("g p n t -> p g (n t)").bitcast(I32)
+            nc.sync.dma_start(out=code[h][:].bitcast(I32), in_=src[:, :, h * DOC_HALF : (h + 1) * DOC_HALF])
+
+        cross_cols = kept("cross_cols", [P, DOCS // P], BF16)
+        identity = kept("identity", [P, P], F32)
+        make_identity(nc, identity[:])
+        nc.scalar.dma_start(out=cross_cols[:], in_=cross.rearrange("(p c) -> p c", p=P))
+        for half in range(2):
+            load_words(nc.sync, book_raw[half], book_words, half)
+            load_scale_rows(book_scale_raw[half], book_scales, half)
+            if half == 1:
+                nc.sync.dma_start(out=norm_cols[:], in_=norms.rearrange("(g p t) -> p g t", p=P, t=PACK))
+                nc.sync.dma_start(out=cap_cols[:], in_=caps.rearrange("(g p t) -> p g t", p=P, t=PACK))
+            load_words(nc.sync, query[half], query_words, half)
+            load_scale_rows(query_scale[half], query_scales, half)
+        load_code_words(0)
+        load_scale_rows(code_scale, code_scales, 0)
+        load_code_words(1)
+
+        cross_pairs = cross_cols[:].bitcast(F32)
+        pairs = cross_pairs.shape[1]
+        per_bank = BANK // P
+        spread_pairs = cross_rows[:].bitcast(F32).rearrange("f (p w) -> f p w", w=pairs)
+        for first in range(0, pairs, per_bank):
+            bank = BANKS - 3 + first // per_bank
+            spread = psum.tile([P, per_bank, P], F32, name="spread%d" % bank, tag="acc%d" % bank)
+            for w in range(per_bank):
+                column = cross_pairs[:, first + w : first + w + 1].to_broadcast([P, P])
+                nc.tensor.transpose(spread[:, w, :], column, identity[:])
+            nc.scalar.copy(out=spread_pairs[:, :, first : first + per_bank], in_=spread[:].rearrange("f w p -> f p w"))
 
         def permute_books(u):
             g, t = divmod(u, PACK)
@@ -121,7 +159,7 @@ def tile_additive_quantisation_scan_s4_kernel(
             )
             nc.vector.tensor_copy(
                 out=book_scale[u][:],
-                in_=book_scale_raw[:].rearrange("p d (g c t) -> p d g c t", g=J_PASSES, t=PACK)[:, :, g, :, t],
+                in_=book_scale_raw[g][:].rearrange("p d (c t) -> p d c t", t=PACK)[:, :, :, t],
             )
 
         def table_matmul(acc, c, u):
@@ -154,8 +192,8 @@ def tile_additive_quantisation_scan_s4_kernel(
             first = i * P - CHUNK_START[c]
             src = table_rows[c][:].rearrange("p (g t) m -> p g t m", t=PACK)[:, :, :, first : first + P]
             nc.scalar.copy(
-                out=table_words[i][:].rearrange("p g (a r) t -> p g a t r", r=RUN),
-                in_=src.rearrange("p g t (a r) -> p g a t r", r=RUN),
+                out=table_words[i][:],
+                in_=src.rearrange("p g t m -> p g m t"),
             )
 
         def quantize(i):
@@ -198,7 +236,7 @@ def tile_additive_quantisation_scan_s4_kernel(
         quantize_at = {steps.index(("scan", i - 1, 1)): (i,) for i in range(1, M_TILES)}
         quantize_at[UNITS + 1] = (0,)
 
-        for u in range(PERMUTE_LEAD):
+        for u in range(UNITS):
             permute_books(u)
         pending = None
         for s, (kind, a, b) in enumerate(steps):
@@ -216,8 +254,6 @@ def tile_additive_quantisation_scan_s4_kernel(
             if pending is not None:
                 truncate(*pending)
                 pending = None
-            if s + PERMUTE_LEAD - 1 < UNITS and s >= 1:
-                permute_books(s + PERMUTE_LEAD - 1)
             for i in interleave_at.get(s, ()):
                 interleave(i)
             if kind == "table" and a == 0:

from contextlib import ExitStack

import concourse.mybir as mybir
from concourse.masks import make_identity

M, D, J, DOCS = 1024, 1536, 1024, 2048
FLOPS = 2 * M * D * J + 2 * M * J * DOCS

F32 = mybir.dt.float32
BF16 = mybir.dt.bfloat16
I32 = mybir.dt.int32
U32 = mybir.dt.uint32
U8 = mybir.dt.uint8
FP8X4 = mybir.dt.float8_e4m3fn_x4
FP4X4 = mybir.dt.float4_e2m1fn_x4
ALU = mybir.AluOpType

P = 128
PACK = 4
K_PASS = P * PACK
D_PASSES = D // K_PASS
J_PASSES = J // K_PASS
BANK = 512
BANKS = 8
HALVES = M // BANK
CHUNK_START = (0, 512, 768)
CHUNK_WIDTH = (512, 256, 256)
UNITS = J_PASSES * PACK
M_TILES = M // P
DOC_BLOCKS = DOCS // BANK
DOC_HALF = DOCS // 2
WARM_PASSES = 14


def table_steps(c):
    per_bank = BANK // CHUNK_WIDTH[c]
    return [("table", c, u) for u in range(0, UNITS, per_bank)]


def tensor_steps():
    steps = table_steps(0) + table_steps(1)
    late = table_steps(2)
    for i in range(M_TILES):
        steps.extend(("scan", i, n) for n in range(DOC_BLOCKS))
        steps.extend(late[i : i + 1])
    return steps


def chunk_of(i):
    return max(c for c in range(len(CHUNK_START)) if CHUNK_START[c] <= i * P)


def tile_additive_quantisation_scan_s4_kernel(
    tc, query_words, query_scales, book_words, book_scales, norms, caps, code_words, code_scales, cross, out
):
    nc = tc.nc
    with ExitStack() as ctx:
        keep = ctx.enter_context(tc.tile_pool(name="keep", bufs=1))
        stage = ctx.enter_context(tc.tile_pool(name="stage", bufs=UNITS))
        psum = ctx.enter_context(tc.psum_pool(name="psum", bufs=1))
        ctx.enter_context(tc.manual_schedule())

        def kept(name, shape, dtype):
            return keep.tile(shape, dtype, name=name, align_bytes=64)

        book_raw = [kept("book_raw%d" % g, [P, D_PASSES, 2 * K_PASS], U8) for g in range(J_PASSES)]
        book_scale_raw = [kept("book_scale_raw%d" % g, [P, D_PASSES, K_PASS], U8) for g in range(J_PASSES)]
        book = [kept("book%d" % u, [P, D_PASSES, 2 * P], U8) for u in range(UNITS)]
        book_scale = [kept("book_scale%d" % u, [P, D_PASSES, P], U8) for u in range(UNITS)]
        query = [kept("query%d" % c, [P, D_PASSES, 2 * BANK], U8) for c in range(HALVES)]
        query_scale = [kept("query_scale%d" % c, [P, D_PASSES, BANK], U8) for c in range(HALVES)]
        code = [kept("code%d" % h, [P, J_PASSES, DOC_HALF], U32) for h in range(2)]
        code_scale = kept("code_scale", [P, J_PASSES, DOCS], U8)
        norm_cols = kept("norm_cols", [P, J_PASSES, PACK], BF16)
        cap_cols = kept("cap_cols", [P, J_PASSES, PACK], BF16)
        cross_rows = kept("cross_rows", [P, DOCS], BF16)
        table_rows = [kept("table_rows%d" % c, [P, UNITS, w], BF16) for c, w in enumerate(CHUNK_WIDTH)]
        table_words = [kept("table_words%d" % i, [P, J_PASSES, P, PACK], BF16) for i in range(M_TILES)]
        table_code = [kept("table_code%d" % i, [P, J_PASSES, P], U32) for i in range(M_TILES)]
        table_scale = [kept("table_scale%d" % i, [P, J_PASSES, P], U8) for i in range(M_TILES)]
        result = [kept("result%d" % i, [P, DOCS], F32) for i in range(M_TILES)]

        def load_words(queue, tile, words, part):
            width = tile.shape[2] // 4
            src = words.bitcast(I32).rearrange("g p w -> p g w")
            queue.dma_start(out=tile[:].bitcast(I32), in_=src[:, :, part * width : (part + 1) * width])

        def load_scale_rows(tile, scales, part):
            width = tile.shape[2] // 4
            src = scales.bitcast(I32).rearrange("g q w -> q g w")
            for quadrant in range(4):
                nc.sync.dma_start(
                    out=tile[:].bitcast(I32)[32 * quadrant : 32 * quadrant + 4],
                    in_=src[4 * quadrant : 4 * quadrant + 4, :, part * width : (part + 1) * width],
                )

        def clear(engine, plane):
            engine.memset(plane[:].bitcast(I32), 0)

        clear(nc.vector, book_scale_raw[0])
        clear(nc.vector, query_scale[0])
        warm_in = kept("warm_in", [P, PACK * P], BF16)
        warm_code = kept("warm_code", [P, P], U32)
        warm_scale = kept("warm_scale", [P, P], U8)
        nc.vector.memset(warm_in[:], 0.0)
        nc.vector.quantize_mx(out=warm_code[:].bitcast(FP8X4), scales=warm_scale[:], in_=warm_in[:])
        warm_acc = psum.tile([P, BANK], F32, name="warm_acc", tag="acc%d" % (BANKS - 1))
        for k in range(WARM_PASSES):
            nc.tensor.matmul_mx(
                out=warm_acc[:, :P],
                lhsT=warm_code[:].bitcast(FP8X4),
                lhsT_scale=warm_scale[:],
                rhs=warm_code[:].bitcast(FP8X4),
                rhs_scale=warm_scale[:],
                start=(k == 0),
                stop=(k == WARM_PASSES - 1),
            )
        clear(nc.vector, book_scale_raw[1])
        clear(nc.vector, query_scale[1])
        clear(nc.vector, code_scale)

        def load_code_words(h):
            src = code_words.rearrange("g p n t -> p g (n t)").bitcast(I32)
            nc.sync.dma_start(out=code[h][:].bitcast(I32), in_=src[:, :, h * DOC_HALF : (h + 1) * DOC_HALF])

        cross_cols = kept("cross_cols", [P, DOCS // P], BF16)
        identity = kept("identity", [P, P], F32)
        make_identity(nc, identity[:])
        nc.scalar.dma_start(out=cross_cols[:], in_=cross.rearrange("(p c) -> p c", p=P))
        for half in range(2):
            load_words(nc.sync, book_raw[half], book_words, half)
            load_scale_rows(book_scale_raw[half], book_scales, half)
            if half == 1:
                nc.sync.dma_start(out=norm_cols[:], in_=norms.rearrange("(g p t) -> p g t", p=P, t=PACK))
                nc.sync.dma_start(out=cap_cols[:], in_=caps.rearrange("(g p t) -> p g t", p=P, t=PACK))
            load_words(nc.sync, query[half], query_words, half)
            load_scale_rows(query_scale[half], query_scales, half)
        load_code_words(0)
        load_scale_rows(code_scale, code_scales, 0)
        load_code_words(1)

        cross_pairs = cross_cols[:].bitcast(F32)
        pairs = cross_pairs.shape[1]
        per_bank = BANK // P
        spread_pairs = cross_rows[:].bitcast(F32).rearrange("f (p w) -> f p w", w=pairs)
        for first in range(0, pairs, per_bank):
            bank = BANKS - 3 + first // per_bank
            spread = psum.tile([P, per_bank, P], F32, name="spread%d" % bank, tag="acc%d" % bank)
            for w in range(per_bank):
                column = cross_pairs[:, first + w : first + w + 1].to_broadcast([P, P])
                nc.tensor.transpose(spread[:, w, :], column, identity[:])
            nc.scalar.copy(out=spread_pairs[:, :, first : first + per_bank], in_=spread[:].rearrange("f w p -> f p w"))

        def permute_books(u):
            g, t = divmod(u, PACK)
            nc.vector.tensor_copy(
                out=book[u][:].rearrange("p d (c b) -> p d c b", b=2),
                in_=book_raw[g][:].rearrange("p d (c t b) -> p d c t b", t=PACK, b=2)[:, :, :, t, :],
            )
            nc.vector.tensor_copy(
                out=book_scale[u][:],
                in_=book_scale_raw[g][:].rearrange("p d (c t) -> p d c t", t=PACK)[:, :, :, t],
            )

        def table_matmul(acc, c, u):
            half, first = divmod(CHUNK_START[c], BANK)
            last = first + CHUNK_WIDTH[c]
            for d in range(D_PASSES):
                nc.tensor.matmul_mx(
                    out=acc,
                    lhsT=book[u][:, d, :].bitcast(FP4X4),
                    lhsT_scale=book_scale[u][:, d, :],
                    rhs=query[half][:, d, 2 * first : 2 * last].bitcast(FP4X4),
                    rhs_scale=query_scale[half][:, d, first:last],
                    start=(d == 0),
                    stop=(d == D_PASSES - 1),
                )

        def truncate(dots, c, u):
            g, t = divmod(u, PACK)
            nc.vector.tensor_scalar(
                out=table_rows[c][:, u, :],
                in0=dots,
                scalar1=norm_cols[:, g, t : t + 1],
                scalar2=cap_cols[:, g, t : t + 1],
                op0=ALU.add,
                op1=ALU.min,
            )

        def interleave(i):
            c = chunk_of(i)
            first = i * P - CHUNK_START[c]
            src = table_rows[c][:].rearrange("p (g t) m -> p g t m", t=PACK)[:, :, :, first : first + P]
            nc.scalar.copy(
                out=table_words[i][:],
                in_=src.rearrange("p g t m -> p g m t"),
            )

        def quantize(i):
            nc.vector.quantize_mx(
                out=table_code[i][:].rearrange("p g m -> p (g m)").bitcast(FP8X4),
                scales=table_scale[i][:].rearrange("p g m -> p (g m)"),
                in_=table_words[i][:].rearrange("p g m t -> p (g m t)"),
            )

        def scan_matmul(acc, i, n):
            h, k = divmod(n, DOC_HALF // BANK)
            for g in range(J_PASSES):
                nc.tensor.matmul_mx(
                    out=acc[:],
                    lhsT=table_code[i][:, g, :].bitcast(FP8X4),
                    lhsT_scale=table_scale[i][:, g, :],
                    rhs=code[h][:, g, k * BANK : (k + 1) * BANK].bitcast(FP8X4),
                    rhs_scale=code_scale[:, g, n * BANK : (n + 1) * BANK],
                    start=(g == 0),
                    stop=(g == J_PASSES - 1),
                )

        def add_cross_and_store(acc, i, n):
            cols = slice(n * BANK, (n + 1) * BANK)
            if n == 0 and i < M_TILES - 2:
                nc.scalar.copy(out=result[i][:, cols], in_=acc[:])
                nc.gpsimd.tensor_tensor(
                    out=result[i][:, cols], in0=result[i][:, cols], in1=cross_rows[:, cols], op=ALU.add
                )
            else:
                nc.vector.tensor_tensor(out=result[i][:, cols], in0=acc[:], in1=cross_rows[:, cols], op=ALU.add)
            blocks = 1 if i == M_TILES - 1 else 2
            if (n + 1) % blocks == 0:
                done = slice((n + 1 - blocks) * BANK, (n + 1) * BANK)
                nc.sync.dma_start(out=out[i * P : (i + 1) * P, done], in_=result[i][:, done])

        steps = tensor_steps()
        interleave_at = {steps.index(("scan", i - 2, 0)): (i,) for i in range(2, M_TILES)}
        interleave_at[UNITS] = (0, 1)
        quantize_at = {steps.index(("scan", i - 1, 1)): (i,) for i in range(1, M_TILES)}
        quantize_at[UNITS + 1] = (0,)

        for u in range(UNITS):
            permute_books(u)
        pending = None
        for s, (kind, a, b) in enumerate(steps):
            for i in quantize_at.get(s, ()):
                quantize(i)
            acc = psum.tile([P, BANK], F32, name="acc%d" % (s % BANKS), tag="acc%d" % (s % BANKS))
            if kind == "table":
                width = CHUNK_WIDTH[a]
                parts = [acc[:, k * width : (k + 1) * width] for k in range(BANK // width)]
                for k, part in enumerate(parts):
                    table_matmul(part, a, b + k)
            else:
                scan_matmul(acc, a, b)
                add_cross_and_store(acc, a, b)
            if pending is not None:
                truncate(*pending)
                pending = None
            for i in interleave_at.get(s, ()):
                interleave(i)
            if kind == "table" and a == 0:
                dots = stage.tile([P, BANK], F32, name="dots")
                nc.scalar.copy(out=dots[:], in_=acc[:])
                pending = (dots[:], a, b)
            elif kind == "table":
                for k, part in enumerate(parts):
                    truncate(part, a, b + k)
